import numpy as np
import ml_dtypes


def mxq(x, axis, fmt="e4m3"):
    dtype, down = {"e4m3": (ml_dtypes.float8_e4m3fn, 7), "e5m2": (ml_dtypes.float8_e5m2, 14)}[fmt]
    v = np.moveaxis(np.asarray(x, np.float32).astype(ml_dtypes.bfloat16).astype(np.float64), axis, -1)
    blocks = v.reshape(v.shape[:-1] + (-1, 32))
    amax = np.abs(blocks).max(-1, keepdims=True)
    byte = np.maximum(np.where(amax > 0, np.frexp(amax)[1] - 1 + 127, 0) - down, 1)
    scale = np.exp2(byte - 127.0)
    codes = (blocks / scale).astype(np.float32).astype(dtype).astype(np.float64)
    return np.moveaxis((codes * scale).reshape(v.shape), -1, axis)


WIDE = False


def mx_kscale(k):
    if not WIDE:
        return np.ones(k)
    levels = np.array([10, -10, 5, -5, 0])
    if k % 512:
        return np.exp2(np.random.permutation(np.resize(levels, k // 32))).repeat(32)
    a = np.empty((k // 512, 16))
    for p in range(k // 512):
        a[p, :8] = np.random.permutation(np.resize(levels, 8))
        for g in range(8):
            far = levels[np.abs(levels - a[p, g]) >= 10]
            a[p, g + 8] = far[np.random.randint(len(far))]
    return np.exp2(a.ravel()).repeat(32)


def f64(x):
    return np.asarray(x).astype(np.float64)


def striped(idx):
    return np.tile(np.asarray(idx).reshape(-1, 16).T, (8, 1)).astype(np.uint16)


def unstriped(offs):
    return offs[:16].T.reshape(-1).astype(np.int64)


def striped8(idx):
    return np.asarray(idx).reshape(8, -1, 16).transpose(0, 2, 1).reshape(128, -1).astype(np.uint16)


def unstriped8(offs):
    return offs.reshape(8, 16, -1).transpose(0, 2, 1).reshape(8, -1).astype(np.int64)


def pick8(x, idx, run):
    r = np.arange(len(x))
    return x[r[:, None], idx[r % (8 * run) // run]]


E2M1 = np.array([0.0, 0.5, 1.0, 1.5, 2.0, 3.0, 4.0, 6.0, -0.0, -0.5, -1.0, -1.5, -2.0, -3.0, -4.0, -6.0])


def pack_weight(w, fmt):
    k, n = w.shape
    w = f64(np.asarray(w, np.float32).astype(ml_dtypes.bfloat16)).reshape(k // 32, 32, n)
    amax = np.abs(w).max(1)
    if fmt == "e4m3":
        byte = np.frexp(amax)[1] - 1 + 127 - 7
    else:
        mant, ex = np.frexp(amax / 6.0)
        byte = np.where(mant > 0.5, ex, ex - 1) + 127
    byte = np.clip(np.where(amax > 0, byte, 1), 1, 254)
    scaled = (w * np.exp2(127.0 - byte)[:, None, :]).reshape(k, n).astype(np.float32)
    by_word = np.ascontiguousarray(scaled.reshape(k // 512, 128, 4, n).transpose(0, 1, 3, 2))
    if fmt == "e4m3":
        words = by_word.astype(ml_dtypes.float8_e4m3fn).view(np.uint8)
    else:
        c = by_word.astype(ml_dtypes.float4_e2m1fn).view(np.uint8) & 0xF
        words = (c[..., 0::2] | (c[..., 1::2] << 4)).reshape(k // 512, 128, 2 * n)
    return np.ascontiguousarray(words), np.ascontiguousarray(byte.astype(np.uint8).reshape(k // 512, 16, n))


def unpack_weight(words, scales, fmt):
    g, _, n = scales.shape
    words = np.ascontiguousarray(words).reshape(g, 128, n, -1)
    if fmt == "e4m3":
        vals = words.view(ml_dtypes.float8_e4m3fn).astype(np.float64)
    else:
        nib = np.empty((g, 128, n, 4), np.uint8)
        nib[..., 0::2] = words & 0xF
        nib[..., 1::2] = words >> 4
        vals = E2M1[nib]
    vals = vals * np.repeat(np.exp2(scales.astype(np.float64) - 127.0), 8, axis=1)[..., None]
    return vals.transpose(0, 1, 3, 2).reshape(g * 512, n)


def bf(x):
    return np.asarray(x, np.float32).astype(ml_dtypes.bfloat16)


def planes(Y):
    r, m = Y.shape
    b = f64(bf(Y)).reshape(r // 32, 32, m)
    amax = np.abs(b).max(1)
    byte = np.clip(np.where(amax > 0, np.frexp(amax)[1] - 1 + 127 - 7, 1), 1, 254)
    codes = (b * np.exp2(127.0 - byte)[:, None, :]).reshape(r, m).astype(np.float32).astype(ml_dtypes.float8_e4m3fn).view(np.uint8)
    words = codes.reshape(r // 512, 128, 4, m).transpose(0, 1, 3, 2)
    return np.ascontiguousarray(words), np.ascontiguousarray(byte.astype(np.uint8).reshape(r // 512, 16, m))


K, T, J, I, R, N = 512, 1024, 512, 512, 512, 512


def setup_inputs():
    n = np.random.standard_normal
    idx = np.random.permutation(T)[:J]
    idx2 = np.stack([np.random.randint(0, J, I) for _ in range(8)])
    fk = mx_kscale(K)
    fr = mx_kscale(R)
    xtp = pack_weight(n((K, T)) / fk[:, None], "e2m1")
    wap = pack_weight(n((K, R)) * 1 / np.sqrt(K) * fk[:, None] * fr, "e4m3")
    wbp = pack_weight(n((R, N)) * 1 / np.sqrt(R) / fr[:, None], "e2m1")
    return {
        "xt_words": xtp[0],
        "xt_scales": xtp[1],
        "wa_words": wap[0],
        "wa_scales": wap[1],
        "wb_words": wbp[0],
        "wb_scales": wbp[1],
        "rw": (np.random.uniform(0.5, 2.0, (1, I))).astype(np.float32),
        "offs": striped(idx),
        "offs2": striped8(idx2),
    }


def reference(xt_words, xt_scales, wa_words, wa_scales, wb_words, wb_scales, rw, offs, offs2):
    idx = unstriped(offs)
    idx2 = unstriped8(offs2)
    xtu = unpack_weight(xt_words, xt_scales, "e2m1")
    wau = unpack_weight(wa_words, wa_scales, "e4m3")
    wbu = unpack_weight(wb_words, wb_scales, "e2m1")
    xtidxg = xtu[:, idx]
    a = wau.T @ xtidxg
    hid = np.maximum(a, 0.0)
    hididx2q = mxq(pick8(hid, idx2, 64), 0, "e4m3")
    p = wbu.T @ hididx2q
    y = p * f64(rw)
    words, scales = planes(y)
    return y, words, scales

@@ -1,0 +1,206 @@
+from contextlib import ExitStack
+
+import concourse.mybir as mybir
+
+K, T, J, I, R, N = 512, 1024, 512, 512, 512, 512
+FLOPS = 2 * K * R * J + 2 * R * N * I
+
+F32 = mybir.dt.float32
+BF16 = mybir.dt.bfloat16
+I32 = mybir.dt.int32
+U16 = mybir.dt.uint16
+U8 = mybir.dt.uint8
+FP8X4 = mybir.dt.float8_e4m3fn_x4
+FP4X4 = mybir.dt.float4_e2m1fn_x4
+RELU = mybir.ActivationFunctionType.Relu
+MULT = mybir.AluOpType.mult
+
+P = 128
+PACK = 4
+HALF = J // 2
+CHUNKS = (128, 128, 128, 128,)
+
+
+def load_scale_rows(queues, plane, rows):
+    by_row = rows[0].rearrange("(q r) c -> r q c", r=4)
+    for r in range(4):
+        queues[r % 2].dma_start(out=plane[r:P:32, :].bitcast(I32), in_=by_row[r].bitcast(I32))
+
+
+def deal_columns(nc, dealt, natural):
+    nc.vector.tensor_copy(
+        out=dealt.rearrange("p (t m) -> p m t", t=PACK),
+        in_=natural.rearrange("p (m t) -> p m t", t=PACK),
+    )
+
+
+def interleave(copy, grouped, planes):
+    copy(
+        out=grouped.rearrange("p (c i) t -> p c t i", i=4),
+        in_=planes.rearrange("p t (c i) -> p c t i", i=4),
+    )
+
+
+def tile_moe_expert_hidden_slots_swapped_pl_kernel(
+    tc, xt_words, xt_scales, wa_words, wa_scales, wb_words, wb_scales, rw, offs, offs2, out_0, out_1, out_2
+):
+    nc = tc.nc
+    with ExitStack() as ctx:
+        keep = ctx.enter_context(tc.tile_pool(name="keep", bufs=1))
+        psum = ctx.enter_context(tc.psum_pool(name="psum", bufs=1))
+
+        slot_list = keep.tile([P, J // 16], U16, name="slot_list")
+        place_lists = keep.tile([P, I // 16], U16, name="place_lists")
+        x_words = keep.tile([P, 2 * T], U8, name="x_words", align_bytes=64)
+        x_plane = keep.tile([P, T], U8, name="x_plane", align_bytes=64)
+        wa_raw = keep.tile([P, R], I32, name="wa_raw", align_bytes=64)
+        wa_plane_raw = keep.tile([P, R], U8, name="wa_plane_raw", align_bytes=64)
+        wb_raw = keep.tile([P, 2 * N], U8, name="wb_raw", align_bytes=64)
+        wb_plane_raw = keep.tile([P, N], U8, name="wb_plane_raw", align_bytes=64)
+        rw_rows = keep.tile([P, 1, I], F32, name="rw_rows", align_bytes=64)
+
+        for plane in (wa_plane_raw, x_plane, wb_plane_raw):
+            nc.vector.memset(plane[:].bitcast(I32), 0)
+
+        nc.sync.dma_start(slot_list[:], offs)
+        nc.scalar.dma_start(out=x_words[:].bitcast(I32), in_=xt_words[0].bitcast(I32))
+        nc.scalar.dma_start(out=wa_raw[:], in_=wa_words[0].rearrange("p c r -> p (c r)").bitcast(I32))
+        load_scale_rows((nc.sync, nc.sync), wa_plane_raw, wa_scales)
+        load_scale_rows((nc.sync, nc.sync), x_plane, xt_scales)
+        nc.sync.dma_start(place_lists[:], offs2)
+        nc.sync.dma_start(out=wb_raw[:].bitcast(I32), in_=wb_words[0].bitcast(I32))
+        load_scale_rows((nc.sync, nc.sync), wb_plane_raw, wb_scales)
+        nc.sync.dma_start(out=rw_rows[:, 0, :], in_=rw[0].partition_broadcast(P))
+
+        wa_dealt = keep.tile([P, R], I32, name="wa_dealt", align_bytes=64)
+        wa_plane = keep.tile([P, R], U8, name="wa_plane", align_bytes=64)
+        wb_dealt = keep.tile([P, 2 * N], U8, name="wb_dealt", align_bytes=64)
+        wb_plane = keep.tile([P, N], U8, name="wb_plane", align_bytes=64)
+        hid = [keep.tile([P, J], F32, name=f"hid{t}", align_bytes=64) for t in range(PACK)]
+
+        slot_words = keep.tile([P, 2 * J], U8, name="slot_words", align_bytes=64)
+        slot_plane = keep.tile([P, J], U8, name="slot_plane", align_bytes=64)
+        zero_bias = keep.tile([P, 1], F32, name="zero_bias", tag="stage2", align_bytes=64)
+        nc.vector.memset(zero_bias[:], 0.0)
+
+        def gather_words(h):
+            entries = slot_list[:, h * HALF // 16 : (h + 1) * HALF // 16]
+            words = slot_words[:].bitcast(U16)[:, h * HALF : (h + 1) * HALF]
+            nc.vector.tensor_copy(words, x_words[:].bitcast(U16).indirect(entries))
+
+        def gather_plane(h):
+            entries = slot_list[:, h * HALF // 16 : (h + 1) * HALF // 16]
+            nc.vector.tensor_copy(slot_plane[:, h * HALF : (h + 1) * HALF], x_plane[:].indirect(entries))
+
+        def first_layer(t, lo, n, bank):
+            cols = slice(t * P, (t + 1) * P)
+            acc = psum.tile([P, n], F32, name=f"acc{bank}", tag=f"bank{bank}")
+            nc.tensor.matmul_mx(
+                out=acc[:],
+                lhsT=wa_dealt[:, cols].bitcast(FP8X4),
+                lhsT_scale=wa_plane[:, cols],
+                rhs=slot_words[:, 2 * lo : 2 * (lo + n)].bitcast(FP4X4),
+                rhs_scale=slot_plane[:, lo : lo + n],
+                start=True,
+                stop=True,
+            )
+            nc.scalar.activation(hid[t][:, lo : lo + n], acc[:], RELU, bias=zero_bias[:])
+
+        gather_words(0)
+        gather_words(1)
+        deal_columns(nc, wa_dealt[:], wa_raw[:])
+        deal_columns(nc, wa_plane[:], wa_plane_raw[:])
+        gather_plane(0)
+        gather_plane(1)
+        first_layer(0, 0, HALF, 0)
+        first_layer(1, 0, HALF, 1)
+        first_layer(0, HALF, HALF, 2)
+        first_layer(1, HALF, HALF, 3)
+        first_layer(2, 0, J, 4)
+        first_layer(3, 0, J, 5)
+        deal_columns(nc, wb_dealt[:].bitcast(U16), wb_raw[:].bitcast(U16))
+        deal_columns(nc, wb_plane[:], wb_plane_raw[:])
+
+        y_words = keep.tile([P, I], I32, name="y_words", align_bytes=64)
+        y_plane = keep.tile([P, I], U8, name="y_plane", align_bytes=64)
+        out_rows = out_0.rearrange("(p t) i -> p t i", t=PACK)
+        out_words = out_1[0].rearrange("p c r -> p (c r)").bitcast(I32)
+
+        starts = [sum(CHUNKS[:c]) for c in range(len(CHUNKS))]
+        grouped = {}
+        sums = {}
+        y_grouped = {}
+        late = []
+
+        def look_up(c):
+            lo, n = starts[c], CHUNKS[c]
+            entries = place_lists[:, lo // 16 : (lo + n) // 16]
+            picked = keep.tile([P, PACK, n], BF16, name=f"picked{c}", tag=f"stage{c % 3}", align_bytes=64)
+            for t in range(PACK):
+                nc.vector.tensor_copy(picked[:, t, :], hid[t][:].indirect(entries))
+            grouped[c] = keep.tile([P, n, PACK], BF16, name=f"grouped{c}", align_bytes=64)
+            interleave(nc.scalar.copy, grouped[c][:], picked[:])
+
+        def second_layer(c):
+            n = CHUNKS[c]
+            codes = keep.tile([P, n], I32, name=f"codes{c}", align_bytes=64)
+            plane = keep.tile([P, n], U8, name=f"plane{c}", align_bytes=64)
+            nc.vector.quantize_mx(
+                out=codes[:].bitcast(FP8X4), scales=plane[:], in_=grouped[c][:].rearrange("p c t -> p (c t)")
+            )
+            bank = (6 + c) % 8
+            sums[c] = psum.tile([P, PACK, n], F32, name=f"sums{c}", tag=f"bank{bank}")
+            for t in range(PACK):
+                nc.tensor.matmul_mx(
+                    out=sums[c][:, t, :],
+                    lhsT=wb_dealt[:, 2 * t * P : 2 * (t + 1) * P].bitcast(FP4X4),
+                    lhsT_scale=wb_plane[:, t * P : (t + 1) * P],
+                    rhs=codes[:].bitcast(FP8X4),
+                    rhs_scale=plane[:],
+                    start=True,
+                    stop=True,
+                )
+
+        def weigh(c):
+            lo, n = starts[c], CHUNKS[c]
+            y = keep.tile([P, PACK, n], F32, name=f"y{c}", tag=f"stage{(2, 0, 3, 4)[c]}", align_bytes=64)
+            nc.vector.tensor_tensor(y[:], sums[c][:], rw_rows[:, :, lo : lo + n].to_broadcast([P, PACK, n]), MULT)
+            nc.sync.dma_start(out=out_rows[:, :, lo : lo + n], in_=y[:])
+            y_grouped[c] = keep.tile([P, n, PACK], BF16, name=f"y_grouped{c}", align_bytes=64)
+            if c < 3:
+                interleave(nc.scalar.copy, y_grouped[c][:], y[:])
+            else:
+                interleave(nc.scalar.copy, y_grouped[c][:, : n // 2, :], y[:, :, : n // 2])
+                late.append(lambda: interleave(nc.vector.tensor_copy, y_grouped[c][:, n // 2 :, :], y[:, :, n // 2 :]))
+
+        def hand_on(c):
+            lo, n = starts[c], CHUNKS[c]
+            nc.vector.quantize_mx(
+                out=y_words[:, lo : lo + n].bitcast(FP8X4),
+                scales=y_plane[:, lo : lo + n],
+                in_=y_grouped[c][:].rearrange("p c t -> p (c t)"),
+            )
+            if c % 2 == 1:
+                nc.sync.dma_start(out=out_words[:, lo - n : lo + n], in_=y_words[:, lo - n : lo + n])
+
+        for c in range(3):
+            look_up(c)
+        second_layer(0)
+        look_up(3)
+        second_layer(1)
+        second_layer(2)
+        weigh(0)
+        second_layer(3)
+        weigh(1)
+        weigh(2)
+        weigh(3)
+        hand_on(0)
+        hand_on(1)
+        late[0]()
+        hand_on(2)
+        hand_on(3)
+
+        scale_rows = out_2[0].rearrange("(q r) c -> r q c", r=4)
+        for r in range(4):
+            queue = nc.sync if r % 2 == 0 else nc.scalar
+            queue.dma_start(out=scale_rows[r].bitcast(I32), in_=y_plane[r:P:32, :].bitcast(I32))

@@ -22,15 +22,15 @@ CHUNKS = (128, 128, 128, 128,)
 
 
 def load_scale_rows(queues, plane, rows):
-    by_row = rows[0].rearrange("(q r) c -> r q c", r=4)
-    for r in range(4):
-        queues[r % 2].dma_start(out=plane[r:P:32, :].bitcast(I32), in_=by_row[r].bitcast(I32))
+    for q in range(4):
+        four_rows = rows[0][4 * q : 4 * q + 4, :].bitcast(I32)
+        queues[q % 2].dma_start(out=plane[32 * q : 32 * q + 32, :].bitcast(I32), in_=four_rows.partition_broadcast(8))
 
 
-def deal_columns(nc, dealt, natural):
+def deal_columns(nc, dealt, natural, run):
     nc.vector.tensor_copy(
-        out=dealt.rearrange("p (t m) -> p m t", t=PACK),
-        in_=natural.rearrange("p (m t) -> p m t", t=PACK),
+        out=dealt.rearrange("p (t c i) -> p c t i", t=PACK, i=run),
+        in_=natural.rearrange("p (c i t) -> p c t i", t=PACK, i=run),
     )
 
 
@@ -59,17 +59,14 @@ def tile_moe_expert_hidden_slots_swapped_pl_kernel(
         wb_plane_raw = keep.tile([P, N], U8, name="wb_plane_raw", align_bytes=64)
         rw_rows = keep.tile([P, 1, I], F32, name="rw_rows", align_bytes=64)
 
-        for plane in (wa_plane_raw, x_plane, wb_plane_raw):
-            nc.vector.memset(plane[:].bitcast(I32), 0)
-
+        load_scale_rows((nc.sync, nc.scalar), wa_plane_raw, wa_scales)
         nc.sync.dma_start(slot_list[:], offs)
         nc.scalar.dma_start(out=x_words[:].bitcast(I32), in_=xt_words[0].bitcast(I32))
         nc.scalar.dma_start(out=wa_raw[:], in_=wa_words[0].rearrange("p c r -> p (c r)").bitcast(I32))
-        load_scale_rows((nc.sync, nc.sync), wa_plane_raw, wa_scales)
         load_scale_rows((nc.sync, nc.sync), x_plane, xt_scales)
-        nc.sync.dma_start(place_lists[:], offs2)
         nc.sync.dma_start(out=wb_raw[:].bitcast(I32), in_=wb_words[0].bitcast(I32))
         load_scale_rows((nc.sync, nc.sync), wb_plane_raw, wb_scales)
+        nc.sync.dma_start(place_lists[:], offs2)
         nc.sync.dma_start(out=rw_rows[:, 0, :], in_=rw[0].partition_broadcast(P))
 
         wa_dealt = keep.tile([P, R], I32, name="wa_dealt", align_bytes=64)
@@ -106,10 +103,10 @@ def tile_moe_expert_hidden_slots_swapped_pl_kernel(
             )
             nc.scalar.activation(hid[t][:, lo : lo + n], acc[:], RELU, bias=zero_bias[:])
 
+        deal_columns(nc, wa_plane[:], wa_plane_raw[:], 16)
         gather_words(0)
         gather_words(1)
-        deal_columns(nc, wa_dealt[:], wa_raw[:])
-        deal_columns(nc, wa_plane[:], wa_plane_raw[:])
+        deal_columns(nc, wa_dealt[:], wa_raw[:], 4)
         gather_plane(0)
         gather_plane(1)
         first_layer(0, 0, HALF, 0)
@@ -118,8 +115,8 @@ def tile_moe_expert_hidden_slots_swapped_pl_kernel(
         first_layer(1, HALF, HALF, 3)
         first_layer(2, 0, J, 4)
         first_layer(3, 0, J, 5)
-        deal_columns(nc, wb_dealt[:].bitcast(U16), wb_raw[:].bitcast(U16))
-        deal_columns(nc, wb_plane[:], wb_plane_raw[:])
+        deal_columns(nc, wb_dealt[:].bitcast(U16), wb_raw[:].bitcast(U16), 8)
+        deal_columns(nc, wb_plane[:], wb_plane_raw[:], 16)
 
         y_words = keep.tile([P, I], I32, name="y_words", align_bytes=64)
         y_plane = keep.tile([P, I], U8, name="y_plane", align_bytes=64)

from contextlib import ExitStack

import concourse.mybir as mybir

K, T, J, I, R, N = 512, 1024, 512, 512, 512, 512
FLOPS = 2 * K * R * J + 2 * R * N * I

F32 = mybir.dt.float32
BF16 = mybir.dt.bfloat16
I32 = mybir.dt.int32
U16 = mybir.dt.uint16
U8 = mybir.dt.uint8
FP8X4 = mybir.dt.float8_e4m3fn_x4
FP4X4 = mybir.dt.float4_e2m1fn_x4
RELU = mybir.ActivationFunctionType.Relu
MULT = mybir.AluOpType.mult

P = 128
PACK = 4
HALF = J // 2
CHUNKS = (128, 128, 128, 128,)


def load_scale_rows(queues, plane, rows):
    for q in range(4):
        four_rows = rows[0][4 * q : 4 * q + 4, :].bitcast(I32)
        queues[q % 2].dma_start(out=plane[32 * q : 32 * q + 32, :].bitcast(I32), in_=four_rows.partition_broadcast(8))


def deal_columns(nc, dealt, natural, run):
    nc.vector.tensor_copy(
        out=dealt.rearrange("p (t c i) -> p c t i", t=PACK, i=run),
        in_=natural.rearrange("p (c i t) -> p c t i", t=PACK, i=run),
    )


def interleave(copy, grouped, planes):
    copy(
        out=grouped.rearrange("p (c i) t -> p c t i", i=4),
        in_=planes.rearrange("p t (c i) -> p c t i", i=4),
    )


def tile_moe_expert_hidden_slots_swapped_pl_kernel(
    tc, xt_words, xt_scales, wa_words, wa_scales, wb_words, wb_scales, rw, offs, offs2, out_0, out_1, out_2
):
    nc = tc.nc
    with ExitStack() as ctx:
        keep = ctx.enter_context(tc.tile_pool(name="keep", bufs=1))
        psum = ctx.enter_context(tc.psum_pool(name="psum", bufs=1))

        slot_list = keep.tile([P, J // 16], U16, name="slot_list")
        place_lists = keep.tile([P, I // 16], U16, name="place_lists")
        x_words = keep.tile([P, 2 * T], U8, name="x_words", align_bytes=64)
        x_plane = keep.tile([P, T], U8, name="x_plane", align_bytes=64)
        wa_raw = keep.tile([P, R], I32, name="wa_raw", align_bytes=64)
        wa_plane_raw = keep.tile([P, R], U8, name="wa_plane_raw", align_bytes=64)
        wb_raw = keep.tile([P, 2 * N], U8, name="wb_raw", align_bytes=64)
        wb_plane_raw = keep.tile([P, N], U8, name="wb_plane_raw", align_bytes=64)
        rw_rows = keep.tile([P, 1, I], F32, name="rw_rows", align_bytes=64)

        load_scale_rows((nc.sync, nc.scalar), wa_plane_raw, wa_scales)
        nc.sync.dma_start(slot_list[:], offs)
        nc.scalar.dma_start(out=x_words[:].bitcast(I32), in_=xt_words[0].bitcast(I32))
        nc.scalar.dma_start(out=wa_raw[:], in_=wa_words[0].rearrange("p c r -> p (c r)").bitcast(I32))
        load_scale_rows((nc.sync, nc.sync), x_plane, xt_scales)
        nc.sync.dma_start(out=wb_raw[:].bitcast(I32), in_=wb_words[0].bitcast(I32))
        load_scale_rows((nc.sync, nc.sync), wb_plane_raw, wb_scales)
        nc.sync.dma_start(place_lists[:], offs2)
        nc.sync.dma_start(out=rw_rows[:, 0, :], in_=rw[0].partition_broadcast(P))

        wa_dealt = keep.tile([P, R], I32, name="wa_dealt", align_bytes=64)
        wa_plane = keep.tile([P, R], U8, name="wa_plane", align_bytes=64)
        wb_dealt = keep.tile([P, 2 * N], U8, name="wb_dealt", align_bytes=64)
        wb_plane = keep.tile([P, N], U8, name="wb_plane", align_bytes=64)
        hid = [keep.tile([P, J], F32, name=f"hid{t}", align_bytes=64) for t in range(PACK)]

        slot_words = keep.tile([P, 2 * J], U8, name="slot_words", align_bytes=64)
        slot_plane = keep.tile([P, J], U8, name="slot_plane", align_bytes=64)
        zero_bias = keep.tile([P, 1], F32, name="zero_bias", tag="stage2", align_bytes=64)
        nc.vector.memset(zero_bias[:], 0.0)

        def gather_words(h):
            entries = slot_list[:, h * HALF // 16 : (h + 1) * HALF // 16]
            words = slot_words[:].bitcast(U16)[:, h * HALF : (h + 1) * HALF]
            nc.vector.tensor_copy(words, x_words[:].bitcast(U16).indirect(entries))

        def gather_plane(h):
            entries = slot_list[:, h * HALF // 16 : (h + 1) * HALF // 16]
            nc.vector.tensor_copy(slot_plane[:, h * HALF : (h + 1) * HALF], x_plane[:].indirect(entries))

        def first_layer(t, lo, n, bank):
            cols = slice(t * P, (t + 1) * P)
            acc = psum.tile([P, n], F32, name=f"acc{bank}", tag=f"bank{bank}")
            nc.tensor.matmul_mx(
                out=acc[:],
                lhsT=wa_dealt[:, cols].bitcast(FP8X4),
                lhsT_scale=wa_plane[:, cols],
                rhs=slot_words[:, 2 * lo : 2 * (lo + n)].bitcast(FP4X4),
                rhs_scale=slot_plane[:, lo : lo + n],
                start=True,
                stop=True,
            )
            nc.scalar.activation(hid[t][:, lo : lo + n], acc[:], RELU, bias=zero_bias[:])

        deal_columns(nc, wa_plane[:], wa_plane_raw[:], 16)
        gather_words(0)
        gather_words(1)
        deal_columns(nc, wa_dealt[:], wa_raw[:], 4)
        gather_plane(0)
        gather_plane(1)
        first_layer(0, 0, HALF, 0)
        first_layer(1, 0, HALF, 1)
        first_layer(0, HALF, HALF, 2)
        first_layer(1, HALF, HALF, 3)
        first_layer(2, 0, J, 4)
        first_layer(3, 0, J, 5)
        deal_columns(nc, wb_dealt[:].bitcast(U16), wb_raw[:].bitcast(U16), 8)
        deal_columns(nc, wb_plane[:], wb_plane_raw[:], 16)

        y_words = keep.tile([P, I], I32, name="y_words", align_bytes=64)
        y_plane = keep.tile([P, I], U8, name="y_plane", align_bytes=64)
        out_rows = out_0.rearrange("(p t) i -> p t i", t=PACK)
        out_words = out_1[0].rearrange("p c r -> p (c r)").bitcast(I32)

        starts = [sum(CHUNKS[:c]) for c in range(len(CHUNKS))]
        grouped = {}
        sums = {}
        y_grouped = {}
        late = []

        def look_up(c):
            lo, n = starts[c], CHUNKS[c]
            entries = place_lists[:, lo // 16 : (lo + n) // 16]
            picked = keep.tile([P, PACK, n], BF16, name=f"picked{c}", tag=f"stage{c % 3}", align_bytes=64)
            for t in range(PACK):
                nc.vector.tensor_copy(picked[:, t, :], hid[t][:].indirect(entries))
            grouped[c] = keep.tile([P, n, PACK], BF16, name=f"grouped{c}", align_bytes=64)
            interleave(nc.scalar.copy, grouped[c][:], picked[:])

        def second_layer(c):
            n = CHUNKS[c]
            codes = keep.tile([P, n], I32, name=f"codes{c}", align_bytes=64)
            plane = keep.tile([P, n], U8, name=f"plane{c}", align_bytes=64)
            nc.vector.quantize_mx(
                out=codes[:].bitcast(FP8X4), scales=plane[:], in_=grouped[c][:].rearrange("p c t -> p (c t)")
            )
            bank = (6 + c) % 8
            sums[c] = psum.tile([P, PACK, n], F32, name=f"sums{c}", tag=f"bank{bank}")
            for t in range(PACK):
                nc.tensor.matmul_mx(
                    out=sums[c][:, t, :],
                    lhsT=wb_dealt[:, 2 * t * P : 2 * (t + 1) * P].bitcast(FP4X4),
                    lhsT_scale=wb_plane[:, t * P : (t + 1) * P],
                    rhs=codes[:].bitcast(FP8X4),
                    rhs_scale=plane[:],
                    start=True,
                    stop=True,
                )

        def weigh(c):
            lo, n = starts[c], CHUNKS[c]
            y = keep.tile([P, PACK, n], F32, name=f"y{c}", tag=f"stage{(2, 0, 3, 4)[c]}", align_bytes=64)
            nc.vector.tensor_tensor(y[:], sums[c][:], rw_rows[:, :, lo : lo + n].to_broadcast([P, PACK, n]), MULT)
            nc.sync.dma_start(out=out_rows[:, :, lo : lo + n], in_=y[:])
            y_grouped[c] = keep.tile([P, n, PACK], BF16, name=f"y_grouped{c}", align_bytes=64)
            if c < 3:
                interleave(nc.scalar.copy, y_grouped[c][:], y[:])
            else:
                interleave(nc.scalar.copy, y_grouped[c][:, : n // 2, :], y[:, :, : n // 2])
                late.append(lambda: interleave(nc.vector.tensor_copy, y_grouped[c][:, n // 2 :, :], y[:, :, n // 2 :]))

        def hand_on(c):
            lo, n = starts[c], CHUNKS[c]
            nc.vector.quantize_mx(
                out=y_words[:, lo : lo + n].bitcast(FP8X4),
                scales=y_plane[:, lo : lo + n],
                in_=y_grouped[c][:].rearrange("p c t -> p (c t)"),
            )
            if c % 2 == 1:
                nc.sync.dma_start(out=out_words[:, lo - n : lo + n], in_=y_words[:, lo - n : lo + n])

        for c in range(3):
            look_up(c)
        second_layer(0)
        look_up(3)
        second_layer(1)
        second_layer(2)
        weigh(0)
        second_layer(3)
        weigh(1)
        weigh(2)
        weigh(3)
        hand_on(0)
        hand_on(1)
        late[0]()
        hand_on(2)
        hand_on(3)

        scale_rows = out_2[0].rearrange("(q r) c -> r q c", r=4)
        for r in range(4):
            queue = nc.sync if r % 2 == 0 else nc.scalar
            queue.dma_start(out=scale_rows[r].bitcast(I32), in_=y_plane[r:P:32, :].bitcast(I32))
